import numpy as np
import ml_dtypes


def mxq(x, axis, fmt="e4m3"):
    dtype, down = {"e4m3": (ml_dtypes.float8_e4m3fn, 7), "e5m2": (ml_dtypes.float8_e5m2, 14)}[fmt]
    v = np.moveaxis(np.asarray(x, np.float32).astype(ml_dtypes.bfloat16).astype(np.float64), axis, -1)
    blocks = v.reshape(v.shape[:-1] + (-1, 32))
    amax = np.abs(blocks).max(-1, keepdims=True)
    byte = np.maximum(np.where(amax > 0, np.frexp(amax)[1] - 1 + 127, 0) - down, 1)
    scale = np.exp2(byte - 127.0)
    codes = (blocks / scale).astype(np.float32).astype(dtype).astype(np.float64)
    return np.moveaxis((codes * scale).reshape(v.shape), -1, axis)


WIDE = False


def mx_kscale(k):
    if not WIDE:
        return np.ones(k)
    levels = np.array([10, -10, 5, -5, 0])
    if k % 512:
        return np.exp2(np.random.permutation(np.resize(levels, k // 32))).repeat(32)
    a = np.empty((k // 512, 16))
    for p in range(k // 512):
        a[p, :8] = np.random.permutation(np.resize(levels, 8))
        for g in range(8):
            far = levels[np.abs(levels - a[p, g]) >= 10]
            a[p, g + 8] = far[np.random.randint(len(far))]
    return np.exp2(a.ravel()).repeat(32)


def f64(x):
    return np.asarray(x).astype(np.float64)


def striped(idx):
    return np.tile(idx.reshape(-1, 16).T, (8, 1)).astype(np.uint16)


def unstriped(offs):
    return offs[:16].T.reshape(-1).astype(np.int64)


E2M1 = np.array([0.0, 0.5, 1.0, 1.5, 2.0, 3.0, 4.0, 6.0, -0.0, -0.5, -1.0, -1.5, -2.0, -3.0, -4.0, -6.0])


def pack_weight(w, fmt):
    k, n = w.shape
    w = f64(np.asarray(w, np.float32).astype(ml_dtypes.bfloat16)).reshape(k // 32, 32, n)
    amax = np.abs(w).max(1)
    if fmt == "e4m3":
        byte = np.frexp(amax)[1] - 1 + 127 - 7
    else:
        mant, ex = np.frexp(amax / 6.0)
        byte = np.where(mant > 0.5, ex, ex - 1) + 127
    byte = np.clip(np.where(amax > 0, byte, 1), 1, 254)
    scaled = (w * np.exp2(127.0 - byte)[:, None, :]).reshape(k, n).astype(np.float32)
    by_word = np.ascontiguousarray(scaled.reshape(k // 512, 128, 4, n).transpose(0, 1, 3, 2))
    if fmt == "e4m3":
        words = by_word.astype(ml_dtypes.float8_e4m3fn).view(np.uint8)
    else:
        c = by_word.astype(ml_dtypes.float4_e2m1fn).view(np.uint8) & 0xF
        words = (c[..., 0::2] | (c[..., 1::2] << 4)).reshape(k // 512, 128, 2 * n)
    return np.ascontiguousarray(words), np.ascontiguousarray(byte.astype(np.uint8).reshape(k // 512, 16, n))


def unpack_weight(words, scales, fmt):
    g, _, n = scales.shape
    words = np.ascontiguousarray(words).reshape(g, 128, n, -1)
    if fmt == "e4m3":
        vals = words.view(ml_dtypes.float8_e4m3fn).astype(np.float64)
    else:
        nib = np.empty((g, 128, n, 4), np.uint8)
        nib[..., 0::2] = words & 0xF
        nib[..., 1::2] = words >> 4
        vals = E2M1[nib]
    vals = vals * np.repeat(np.exp2(scales.astype(np.float64) - 127.0), 8, axis=1)[..., None]
    return vals.transpose(0, 1, 3, 2).reshape(g * 512, n)


def gelu(v):
    return 0.5 * v * (1.0 + np.tanh(np.sqrt(2.0 / np.pi) * (v + 0.044715 * v**3)))


K, KN, H, N, T, TN, S, P = 1024, 512, 1024, 512, 4096, 2048, 1024, 512

def setup_inputs():
    n = np.random.standard_normal
    s = mx_kscale(K)[:, None]
    s2 = mx_kscale(KN)[:, None]
    u = mx_kscale(H)[:, None]
    d = {}
    d["tab_words"], d["tab_scales"] = pack_weight(n((K, T)) * s, "e4m3")
    d["tab2_words"], d["tab2_scales"] = pack_weight(n((KN, TN)) * s2, "e4m3")
    d["offs"] = striped(np.random.permutation(T)[:S])
    d["offs2"] = striped(np.random.permutation(TN)[:P])
    d["pos1"] = striped(np.random.permutation(S)[:P])
    d["w1"] = (n((K, H)) / K**0.5 / s * u.T).astype(np.float32)
    d["base"] = (0.8 * n((H, S)) * u).astype(np.float32)
    d["wn4_words"], d["wn4_scales"] = pack_weight(n((KN, H)) / KN**0.5 / s2 * u.T, "e2m1")
    d["wgs"] = np.exp(0.3 * n((128, P))).astype(np.float32)
    d["wz"] = (1.2 * n((H, N)) / H**0.5 / u).astype(np.float32)
    d["ws8_words"], d["ws8_scales"] = pack_weight(1.2 * n((H, N)) / H**0.5 / u, "e4m3")
    return d

def reference(tab_words, tab_scales, tab2_words, tab2_scales, offs, offs2, pos1, w1, base,
              wn4_words, wn4_scales, wgs, wz, ws8_words, ws8_scales):
    v = unpack_weight(tab_words, tab_scales, "e4m3")[:, unstriped(offs)]
    v2 = unpack_weight(tab2_words, tab2_scales, "e4m3")[:, unstriped(offs2)]
    a = (mxq(f64(w1), 0, "e4m3").T @ v) - f64(base)
    wn4 = unpack_weight(wn4_words, wn4_scales, "e2m1")
    b = np.abs(wn4.T @ v2)
    placed = np.zeros((H, S))
    placed[:, unstriped(pos1)] = np.tile(f64(wgs), (H // 128, 1)) * b
    z = np.maximum(a, placed)
    y = mxq(f64(wz), 0, "e4m3").T @ mxq(z, 0, "e4m3")
    ws8 = unpack_weight(ws8_words, ws8_scales, "e4m3")
    skip = ws8.T @ mxq(a, 0, "e4m3")
    return y * np.tanh(skip)

@@ -1,0 +1,264 @@
+from contextlib import ExitStack
+
+import concourse.mybir as mybir
+
+K, KN, H, N, T, TN, S, NOTES = 1024, 512, 1024, 512, 4096, 2048, 1024, 512
+FLOPS = 2 * (K * H * S + KN * H * NOTES + 2 * H * N * S)
+
+F32 = mybir.dt.float32
+BF16 = mybir.dt.bfloat16
+I32 = mybir.dt.int32
+U32 = mybir.dt.uint32
+U16 = mybir.dt.uint16
+U8 = mybir.dt.uint8
+E4M3 = mybir.dt.float8_e4m3fn_x4
+E2M1 = mybir.dt.float4_e2m1fn_x4
+ALU = mybir.AluOpType
+ACT = mybir.ActivationFunctionType
+
+P = 128
+PACK = 4
+PASS = P * PACK
+BANK = 512
+PAGES = 6
+
+
+def tile_list_visa_interview_priority_kernel(
+    tc, tab_words, tab_scales, tab2_words, tab2_scales, offs, offs2, pos1, w1, base,
+    wn4_words, wn4_scales, wgs, wz, ws8_words, ws8_scales, out,
+):
+    nc = tc.nc
+    with ExitStack() as ctx:
+        held = ctx.enter_context(tc.tile_pool(name="held", bufs=1))
+        raw_pool = ctx.enter_context(tc.tile_pool(name="raw", bufs=5))
+        woven_pool = ctx.enter_context(tc.tile_pool(name="woven", bufs=7))
+        row_pool = ctx.enter_context(tc.tile_pool(name="row", bufs=8))
+        zrow_pool = ctx.enter_context(tc.tile_pool(name="zrow", bufs=2))
+        first_psum = ctx.enter_context(tc.psum_pool(name="first_psum", bufs=4))
+        second_psum = ctx.enter_context(tc.psum_pool(name="second_psum", bufs=4))
+
+        def keep(name, shape, dtype):
+            return held.tile(shape, dtype, name=name, align_bytes=64)
+
+        def zeroed(name, width, dtype):
+            tile = keep(name, [P, width], dtype)
+            view = tile[:].bitcast(I32) if dtype == U8 else tile[:]
+            nc.vector.memset(view, 0)
+            return tile
+
+        def load_list(name, src):
+            tile = held.tile(list(src.shape), U16, name=name)
+            nc.sync.dma_start(tile[:], src)
+            return tile
+
+        def load_words(name, src):
+            tile = keep(name, [P, src.shape[1]], U32)
+            nc.sync.dma_start(tile[:].bitcast(I32), src.rearrange("p t i -> p (t i)").bitcast(I32))
+            return tile
+
+        def load_scale_rows(tile, src):
+            passes = src.shape[0]
+            for q in range(4):
+                rows = src[:, 4 * q : 4 * q + 4, :] if passes > 1 else src[0, 4 * q : 4 * q + 4, :]
+                nc.sync.dma_start(tile[32 * q : 32 * q + 4 * passes, :].bitcast(I32), rows.bitcast(I32))
+
+        def load_rows(src, g, cols):
+            tile = raw_pool.tile([P, PACK, BANK], F32, name="raw")
+            rows = src[g * PASS : (g + 1) * PASS, cols]
+            nc.sync.dma_start(tile[:], rows.rearrange("(p t) c -> p t c", t=PACK))
+            return tile
+
+        def weave(planes, width):
+            woven = woven_pool.tile([P, PACK * BANK], BF16, name="woven", align_bytes=64)
+            nc.scalar.copy(
+                woven[:, : PACK * width].rearrange("p (c i t) -> p c t i", i=4, t=PACK),
+                planes.rearrange("p t (c i) -> p c t i", i=4),
+            )
+            return woven[:, : PACK * width]
+
+        def quantise(name, woven):
+            width = woven.shape[1] // PACK
+            codes = keep(name + "_codes", [P, width], U32)
+            scales = keep(name + "_scales", [P, width], U8)
+            nc.vector.quantize_mx(out=codes[:].bitcast(E4M3), scales=scales[:], in_=woven)
+            return codes, scales
+
+        def gather(name, table, entries, dtype):
+            picked = keep(name, [P, 16 * entries.shape[1]], dtype)
+            nc.vector.tensor_copy(picked[:], table[:].indirect(entries))
+            return picked
+
+        tab2_scale_rows = zeroed("tab2_scale_rows", TN, U8)
+        wn4_scale_rows = zeroed("wn4_scale_rows", H, U8)
+        idx2 = load_list("idx2", offs2)
+        wn4_raw = keep("wn4_raw", [P, 2 * H], U8)
+        nc.sync.dma_start(wn4_raw[:].bitcast(I32), wn4_words[0].bitcast(I32))
+        tab2_codes = load_words("tab2_codes", tab2_words[0])
+        load_scale_rows(tab2_scale_rows, tab2_scales)
+        load_scale_rows(wn4_scale_rows, wn4_scales)
+        wgs_dealt = keep("wgs_dealt", [P, PACK, NOTES], F32)
+        for q in range(4):
+            nc.sync.dma_start(wgs_dealt[32 * q : 32 * q + 32], wgs.rearrange("(p t) j -> p t j", t=PACK))
+        places = load_list("places", pos1)
+
+        halves = [slice(0, BANK), slice(BANK, 2 * BANK)]
+        w1_raw = {(a, 0): load_rows(w1, a, halves[0]) for a in range(2)}
+        idx = load_list("idx", offs)
+
+        wn4_dealt = keep("wn4_dealt", [P, 2 * H], U8)
+        nc.vector.tensor_copy(
+            wn4_dealt[:].rearrange("p (g t m e) -> p g m t e", g=2, t=PACK, e=2),
+            wn4_raw[:].rearrange("p (g m t e) -> p g m t e", g=2, t=PACK, e=2),
+        )
+        v2_codes = gather("v2_codes", tab2_codes, idx2[:], U32)
+        v2_scales = gather("v2_scales", tab2_scale_rows, idx2[:], U8)
+        wn4_scales_dealt = keep("wn4_scales_dealt", [P, H], U8)
+        nc.vector.tensor_copy(
+            wn4_scales_dealt[:].rearrange("p (g t m) -> p g m t", g=2, t=PACK),
+            wn4_scale_rows[:].rearrange("p (g m t) -> p g m t", g=2, t=PACK),
+        )
+
+        pages = [zeroed("page%d" % i, S, F32) for i in range(2)]
+        tab_scale_rows = zeroed("tab_scale_rows", T, U8)
+        ws8_scale_rows = zeroed("ws8_scale_rows", N, U8)
+        pages.extend([zeroed("page%d" % i, S, F32) for i in range(2, PAGES)])
+
+        load_scale_rows(tab_scale_rows, tab_scales)
+        tab_codes = [load_words("tab_codes%d" % a, tab_words[a]) for a in range(2)]
+        for a in range(2):
+            w1_raw[(a, 1)] = load_rows(w1, a, halves[1])
+        wz_raw = [load_rows(wz, g, slice(0, N)) for g in range(2)]
+        base_rows = {(0, h): load_rows(base, 0, halves[h]) for h in range(2)}
+        load_scale_rows(ws8_scale_rows, ws8_scales)
+        ws8_codes = keep("ws8_codes", [P, 2, N], U32)
+        nc.sync.dma_start(
+            ws8_codes[:].bitcast(I32), ws8_words.rearrange("a p c i -> p a (c i)").bitcast(I32)
+        )
+        for h in range(2):
+            base_rows[(1, h)] = load_rows(base, 1, halves[h])
+
+        notes = []
+        for s in range(2 * PACK):
+            acc = first_psum.tile([P, BANK], F32, name="first")
+            nc.tensor.matmul_mx(
+                out=acc[:],
+                lhsT=wn4_dealt[:, 2 * P * s : 2 * P * (s + 1)].bitcast(E2M1),
+                lhsT_scale=wn4_scales_dealt[:, P * s : P * (s + 1)],
+                rhs=v2_codes[:].bitcast(E4M3),
+                rhs_scale=v2_scales[:],
+                start=True,
+                stop=True,
+            )
+            strength = row_pool.tile([P, BANK], F32, name="row")
+            nc.scalar.activation(strength[:], acc[:], ACT.Abs)
+            notes.append(strength)
+
+        def place(s):
+            nc.vector.tensor_tensor(
+                pages[s % PAGES][:].indirect(places[:]), notes[s][:], wgs_dealt[:, s % PACK, :], ALU.mult
+            )
+
+        for s in range(PAGES):
+            place(s)
+
+        def quantise_w1(a, g):
+            woven = woven_pool.tile([P, PACK * BANK], BF16, name="woven", align_bytes=64)
+            nc.scalar.copy(
+                woven[:].rearrange("p (t m j) -> p m j t", t=PACK, j=PACK),
+                w1_raw[(a, g)][:].rearrange("p j (m t) -> p m j t", t=PACK),
+            )
+            return quantise("w1_%d_%d" % (a, g), woven[:])
+
+        w1_mx = {(a, 0): quantise_w1(a, 0) for a in range(2)}
+        v_codes, v_scales = {}, {}
+        for h in range(2):
+            entries = idx[:, 32 * h : 32 * (h + 1)]
+            v_scales[h] = gather("v_scales%d" % h, tab_scale_rows, entries, U8)
+            for a in range(2):
+                v_codes[(a, h)] = gather("v_codes%d_%d" % (a, h), tab_codes[a], entries, U32)
+        for a in range(2):
+            w1_mx[(a, 1)] = quantise_w1(a, 1)
+        wz_mx = [quantise("wz%d" % g, weave(wz_raw[g][:], N)) for g in range(2)]
+
+        def features(g, h):
+            a_rows = base_rows[(g, h)]
+            for t in range(PACK):
+                acc = first_psum.tile([P, BANK], F32, name="first")
+                cols = slice(P * t, P * (t + 1))
+                for a in range(2):
+                    codes, scales = w1_mx[(a, g)]
+                    nc.tensor.matmul_mx(
+                        out=acc[:],
+                        lhsT=codes[:, cols].bitcast(E4M3),
+                        lhsT_scale=scales[:, cols],
+                        rhs=v_codes[(a, h)][:].bitcast(E4M3),
+                        rhs_scale=v_scales[h][4 * a :, :],
+                        start=(a == 0),
+                        stop=(a == 1),
+                    )
+                nc.vector.tensor_tensor(a_rows[:, t, :], acc[:], a_rows[:, t, :], ALU.subtract)
+
+        def quantise_a_z(g, j0, width):
+            h, c0 = divmod(j0, BANK)
+            a_rows = base_rows[(g, h)][:, :, c0 : c0 + width]
+            a_woven = weave(a_rows, width)
+            z_rows = zrow_pool.tile([P, PACK, BANK], BF16, name="z_rows")
+            for t in range(PACK):
+                page = pages[(PACK * g + t) % PAGES]
+                nc.vector.tensor_tensor(
+                    z_rows[:, t, :width], a_rows[:, t, :], page[:, j0 : j0 + width], ALU.max
+                )
+            z_woven = weave(z_rows[:, :, :width], width)
+            tag = "%d_%d" % (g, j0)
+            return quantise("a" + tag, a_woven), quantise("z" + tag, z_woven)
+
+        def second_stage(j0, width, operands):
+            per_bank = BANK // width
+            for n0 in range(0, N // P, per_bank):
+                skip = second_psum.tile([P, per_bank, width], F32, name="second")
+                y = second_psum.tile([P, per_bank, width], F32, name="second")
+                for acc, which in ((skip, 0), (y, 1)):
+                    for u in range(per_bank):
+                        cols = slice(P * (n0 + u), P * (n0 + u + 1))
+                        for g in range(2):
+                            codes, scales = operands[g][which]
+                            if which == 0:
+                                w_codes, w_scales = ws8_codes[:, g, cols], ws8_scale_rows[4 * g :, cols]
+                            else:
+                                w_codes, w_scales = wz_mx[g][0][:, cols], wz_mx[g][1][:, cols]
+                            nc.tensor.matmul_mx(
+                                out=acc[:, u, :],
+                                lhsT=w_codes.bitcast(E4M3),
+                                lhsT_scale=w_scales,
+                                rhs=codes.bitcast(E4M3),
+                                rhs_scale=scales,
+                                start=(g == 0),
+                                stop=(g == 1),
+                            )
+                gate = row_pool.tile([P, BANK], F32, name="row")
+                nc.scalar.activation(gate[:], skip[:].rearrange("p u j -> p (u j)"), ACT.Tanh)
+                result = row_pool.tile([P, BANK], F32, name="row")
+                nc.vector.tensor_tensor(result[:], y[:].rearrange("p u j -> p (u j)"), gate[:], ALU.mult)
+                rows = out[P * n0 : P * (n0 + per_bank), j0 : j0 + width]
+                nc.sync.dma_start(
+                    rows.rearrange("(u p) j -> p u j", p=P), result[:].rearrange("p (u j) -> p u j", u=per_bank)
+                )
+
+        first_pass = []
+        for h in range(2):
+            features(0, h)
+            first_pass.append(quantise_a_z(0, BANK * h, BANK))
+        for s in range(PAGES, 2 * PACK):
+            place(s)
+
+        for j0, width in ((0, 512), (512, 256), (768, 256)):
+            h, c0 = divmod(j0, BANK)
+            if c0 == 0:
+                features(1, h)
+            last = quantise_a_z(1, j0, width)
+            cols = slice(c0, c0 + width)
+            operands = [
+                [(codes[:, cols], scales[:, cols]) for codes, scales in first_pass[h]],
+                [(codes[:], scales[:]) for codes, scales in last],
+            ]
+            second_stage(j0, width, operands)

@@ -20,7 +20,7 @@ P = 128
 PACK = 4
 PASS = P * PACK
 BANK = 512
-PAGES = 6
+PAGES = 4
 
 
 def tile_list_visa_interview_priority_kernel(
@@ -30,7 +30,7 @@ def tile_list_visa_interview_priority_kernel(
     nc = tc.nc
     with ExitStack() as ctx:
         held = ctx.enter_context(tc.tile_pool(name="held", bufs=1))
-        raw_pool = ctx.enter_context(tc.tile_pool(name="raw", bufs=5))
+        raw_pool = ctx.enter_context(tc.tile_pool(name="raw", bufs=6))
         woven_pool = ctx.enter_context(tc.tile_pool(name="woven", bufs=7))
         row_pool = ctx.enter_context(tc.tile_pool(name="row", bufs=8))
         zrow_pool = ctx.enter_context(tc.tile_pool(name="zrow", bufs=2))
@@ -40,10 +40,10 @@ def tile_list_visa_interview_priority_kernel(
         def keep(name, shape, dtype):
             return held.tile(shape, dtype, name=name, align_bytes=64)
 
-        def zeroed(name, width, dtype):
+        def zeroed(name, width, dtype, engine):
             tile = keep(name, [P, width], dtype)
             view = tile[:].bitcast(I32) if dtype == U8 else tile[:]
-            nc.vector.memset(view, 0)
+            engine.memset(view, 0)
             return tile
 
         def load_list(name, src):
@@ -85,50 +85,60 @@ def tile_list_visa_interview_priority_kernel(
 
         def gather(name, table, entries, dtype):
             picked = keep(name, [P, 16 * entries.shape[1]], dtype)
-            nc.vector.tensor_copy(picked[:], table[:].indirect(entries))
+            nc.vector.tensor_copy(picked[:], table.indirect(entries))
             return picked
 
-        tab2_scale_rows = zeroed("tab2_scale_rows", TN, U8)
-        wn4_scale_rows = zeroed("wn4_scale_rows", H, U8)
+        wn4_scale_rows = zeroed("wn4_scale_rows", H, U8, nc.vector)
+        tab2_scale_rows = zeroed("tab2_scale_rows", TN, U8, nc.vector)
         idx2 = load_list("idx2", offs2)
+        places = load_list("places", pos1)
         wn4_raw = keep("wn4_raw", [P, 2 * H], U8)
         nc.sync.dma_start(wn4_raw[:].bitcast(I32), wn4_words[0].bitcast(I32))
+        load_scale_rows(wn4_scale_rows, wn4_scales)
         tab2_codes = load_words("tab2_codes", tab2_words[0])
         load_scale_rows(tab2_scale_rows, tab2_scales)
-        load_scale_rows(wn4_scale_rows, wn4_scales)
         wgs_dealt = keep("wgs_dealt", [P, PACK, NOTES], F32)
-        for q in range(4):
-            nc.sync.dma_start(wgs_dealt[32 * q : 32 * q + 32], wgs.rearrange("(p t) j -> p t j", t=PACK))
-        places = load_list("places", pos1)
+        wgs_rows = wgs.rearrange("(p t) j -> p t j", t=PACK)
+        for planes in (slice(0, 1), slice(1, PACK)):
+            for q in range(4):
+                nc.sync.dma_start(wgs_dealt[32 * q : 32 * q + 32, planes, :], wgs_rows[:, planes, :])
 
         halves = [slice(0, BANK), slice(BANK, 2 * BANK)]
         w1_raw = {(a, 0): load_rows(w1, a, halves[0]) for a in range(2)}
         idx = load_list("idx", offs)
 
-        wn4_dealt = keep("wn4_dealt", [P, 2 * H], U8)
-        nc.vector.tensor_copy(
-            wn4_dealt[:].rearrange("p (g t m e) -> p g m t e", g=2, t=PACK, e=2),
-            wn4_raw[:].rearrange("p (g m t e) -> p g m t e", g=2, t=PACK, e=2),
-        )
-        v2_codes = gather("v2_codes", tab2_codes, idx2[:], U32)
-        v2_scales = gather("v2_scales", tab2_scale_rows, idx2[:], U8)
-        wn4_scales_dealt = keep("wn4_scales_dealt", [P, H], U8)
-        nc.vector.tensor_copy(
-            wn4_scales_dealt[:].rearrange("p (g t m) -> p g m t", g=2, t=PACK),
-            wn4_scale_rows[:].rearrange("p (g m t) -> p g m t", g=2, t=PACK),
-        )
+        def deal_wn4(g):
+            nc.vector.tensor_copy(
+                wn4_codes[:].bitcast(U16).rearrange("p (t m) -> p t m", t=PACK),
+                wn4_raw[:, 2 * PASS * g : 2 * PASS * (g + 1)].bitcast(U16).rearrange("p (m t) -> p t m", t=PACK),
+            )
+            nc.vector.tensor_copy(
+                wn4_dealt_scales[:].rearrange("p (t m) -> p t m", t=PACK),
+                wn4_scale_rows[:, PASS * g : PASS * (g + 1)].rearrange("p (m t) -> p t m", t=PACK),
+            )
 
-        pages = [zeroed("page%d" % i, S, F32) for i in range(2)]
-        tab_scale_rows = zeroed("tab_scale_rows", T, U8)
-        ws8_scale_rows = zeroed("ws8_scale_rows", N, U8)
-        pages.extend([zeroed("page%d" % i, S, F32) for i in range(2, PAGES)])
+        wn4_codes = keep("wn4_codes", [P, 2 * PASS], U8)
+        wn4_dealt_scales = keep("wn4_dealt_scales", [P, PASS], U8)
+        deal_wn4(0)
+        v2_codes = keep("v2_codes", [P, NOTES], U32)
+        v2_scales = keep("v2_scales", [P, NOTES], U8)
+        note_halves = [(slice(256 * u, 256 * (u + 1)), slice(16 * u, 16 * (u + 1))) for u in range(2)]
+        for cols, entries in note_halves:
+            nc.vector.tensor_copy(v2_codes[:, cols], tab2_codes[:].indirect(idx2[:, entries]))
+            nc.vector.tensor_copy(v2_scales[:, cols], tab2_scale_rows[:].indirect(idx2[:, entries]))
+
+        pages = [zeroed("page%d" % i, S, F32, nc.vector) for i in range(2)]
+        tab_scale_rows = zeroed("tab_scale_rows", T, U8, nc.gpsimd)
+        ws8_scale_rows = zeroed("ws8_scale_rows", N, U8, nc.vector)
+        pages.extend([zeroed("page%d" % i, S, F32, nc.gpsimd) for i in range(2, PAGES)])
 
         load_scale_rows(tab_scale_rows, tab_scales)
-        tab_codes = [load_words("tab_codes%d" % a, tab_words[a]) for a in range(2)]
+        tab_codes = keep("tab_codes", [P, 2, T], U32)
+        nc.sync.dma_start(tab_codes[:].bitcast(I32), tab_words.rearrange("a p t i -> p a (t i)").bitcast(I32))
         for a in range(2):
             w1_raw[(a, 1)] = load_rows(w1, a, halves[1])
-        wz_raw = [load_rows(wz, g, slice(0, N)) for g in range(2)]
         base_rows = {(0, h): load_rows(base, 0, halves[h]) for h in range(2)}
+        wz_raw = [load_rows(wz, g, slice(0, N)) for g in range(2)]
         load_scale_rows(ws8_scale_rows, ws8_scales)
         ws8_codes = keep("ws8_codes", [P, 2, N], U32)
         nc.sync.dma_start(
@@ -138,25 +148,33 @@ def tile_list_visa_interview_priority_kernel(
             base_rows[(1, h)] = load_rows(base, 1, halves[h])
 
         notes = []
+        all_notes = [(slice(0, NOTES), slice(0, NOTES // 16))]
         for s in range(2 * PACK):
-            acc = first_psum.tile([P, BANK], F32, name="first")
-            nc.tensor.matmul_mx(
-                out=acc[:],
-                lhsT=wn4_dealt[:, 2 * P * s : 2 * P * (s + 1)].bitcast(E2M1),
-                lhsT_scale=wn4_scales_dealt[:, P * s : P * (s + 1)],
-                rhs=v2_codes[:].bitcast(E4M3),
-                rhs_scale=v2_scales[:],
-                start=True,
-                stop=True,
-            )
+            if s == PACK:
+                deal_wn4(1)
             strength = row_pool.tile([P, BANK], F32, name="row")
-            nc.scalar.activation(strength[:], acc[:], ACT.Abs)
+            for cols, entries in note_halves if s == 0 else all_notes:
+                acc = first_psum.tile([P, BANK], F32, name="first")
+                nc.tensor.matmul_mx(
+                    out=acc[:, cols],
+                    lhsT=wn4_codes[:, 2 * P * (s % PACK) : 2 * P * (s % PACK + 1)].bitcast(E2M1),
+                    lhsT_scale=wn4_dealt_scales[:, P * (s % PACK) : P * (s % PACK + 1)],
+                    rhs=v2_codes[:, cols].bitcast(E4M3),
+                    rhs_scale=v2_scales[:, cols],
+                    start=True,
+                    stop=True,
+                )
+                nc.scalar.activation(strength[:, cols], acc[:, cols], ACT.Abs)
             notes.append(strength)
 
         def place(s):
-            nc.vector.tensor_tensor(
-                pages[s % PAGES][:].indirect(places[:]), notes[s][:], wgs_dealt[:, s % PACK, :], ALU.mult
-            )
+            for cols, entries in note_halves if s == 0 else all_notes:
+                nc.vector.tensor_tensor(
+                    pages[s % PAGES][:].indirect(places[:, entries]),
+                    notes[s][:, cols],
+                    wgs_dealt[:, s % PACK, cols],
+                    ALU.mult,
+                )
 
         for s in range(PAGES):
             place(s)
@@ -173,12 +191,12 @@ def tile_list_visa_interview_priority_kernel(
         v_codes, v_scales = {}, {}
         for h in range(2):
             entries = idx[:, 32 * h : 32 * (h + 1)]
-            v_scales[h] = gather("v_scales%d" % h, tab_scale_rows, entries, U8)
+            v_scales[h] = gather("v_scales%d" % h, tab_scale_rows[:], entries, U8)
             for a in range(2):
-                v_codes[(a, h)] = gather("v_codes%d_%d" % (a, h), tab_codes[a], entries, U32)
+                v_codes[(a, h)] = gather("v_codes%d_%d" % (a, h), tab_codes[:, a, :], entries, U32)
+
         for a in range(2):
             w1_mx[(a, 1)] = quantise_w1(a, 1)
-        wz_mx = [quantise("wz%d" % g, weave(wz_raw[g][:], N)) for g in range(2)]
 
         def features(g, h):
             a_rows = base_rows[(g, h)]
@@ -250,6 +268,7 @@ def tile_list_visa_interview_priority_kernel(
             first_pass.append(quantise_a_z(0, BANK * h, BANK))
         for s in range(PAGES, 2 * PACK):
             place(s)
+        wz_mx = [quantise("wz%d" % g, weave(wz_raw[g][:], N)) for g in range(2)]
 
         for j0, width in ((0, 512), (512, 256), (768, 256)):
             h, c0 = divmod(j0, BANK)

@@ -1,6 +1,7 @@
 from contextlib import ExitStack
 
 import concourse.mybir as mybir
+from concourse.masks import make_identity
 
 K, KN, H, N, T, TN, S, NOTES = 1024, 512, 1024, 512, 4096, 2048, 1024, 512
 FLOPS = 2 * (K * H * S + KN * H * NOTES + 2 * H * N * S)
@@ -20,7 +21,7 @@ P = 128
 PACK = 4
 PASS = P * PACK
 BANK = 512
-PAGES = 4
+PAGES = 6
 
 
 def tile_list_visa_interview_priority_kernel(
@@ -30,18 +31,22 @@ def tile_list_visa_interview_priority_kernel(
     nc = tc.nc
     with ExitStack() as ctx:
         held = ctx.enter_context(tc.tile_pool(name="held", bufs=1))
-        raw_pool = ctx.enter_context(tc.tile_pool(name="raw", bufs=6))
-        woven_pool = ctx.enter_context(tc.tile_pool(name="woven", bufs=7))
-        row_pool = ctx.enter_context(tc.tile_pool(name="row", bufs=8))
-        zrow_pool = ctx.enter_context(tc.tile_pool(name="zrow", bufs=2))
-        first_psum = ctx.enter_context(tc.psum_pool(name="first_psum", bufs=4))
-        second_psum = ctx.enter_context(tc.psum_pool(name="second_psum", bufs=4))
+        psum = ctx.enter_context(tc.psum_pool(name="psum", bufs=1))
+        turns = {}
 
-        def keep(name, shape, dtype):
-            return held.tile(shape, dtype, name=name, align_bytes=64)
+        def in_turn(pool, ring, slots, shape, dtype):
+            turn = turns.get(ring, 0)
+            turns[ring] = turn + 1
+            name = "%s%d" % (ring, turn % slots)
+            if pool is psum:
+                return pool.tile(shape, dtype, name=name, tag=name)
+            return pool.tile(shape, dtype, name=name, tag=name, align_bytes=64)
 
-        def zeroed(name, width, dtype, engine):
-            tile = keep(name, [P, width], dtype)
+        def keep(name, shape, dtype, slot=""):
+            return held.tile(shape, dtype, name=name, tag=slot or name, align_bytes=64)
+
+        def zeroed(name, width, dtype, engine, slot=""):
+            tile = keep(name, [P, width], dtype, slot)
             view = tile[:].bitcast(I32) if dtype == U8 else tile[:]
             engine.memset(view, 0)
             return tile
@@ -51,25 +56,20 @@ def tile_list_visa_interview_priority_kernel(
             nc.sync.dma_start(tile[:], src)
             return tile
 
-        def load_words(name, src):
-            tile = keep(name, [P, src.shape[1]], U32)
-            nc.sync.dma_start(tile[:].bitcast(I32), src.rearrange("p t i -> p (t i)").bitcast(I32))
-            return tile
-
-        def load_scale_rows(tile, src):
+        def load_scale_rows(tile, src, queues):
             passes = src.shape[0]
             for q in range(4):
                 rows = src[:, 4 * q : 4 * q + 4, :] if passes > 1 else src[0, 4 * q : 4 * q + 4, :]
-                nc.sync.dma_start(tile[32 * q : 32 * q + 4 * passes, :].bitcast(I32), rows.bitcast(I32))
+                queues[q].dma_start(tile[32 * q : 32 * q + 4 * passes, :].bitcast(I32), rows.bitcast(I32))
 
         def load_rows(src, g, cols):
-            tile = raw_pool.tile([P, PACK, BANK], F32, name="raw")
+            tile = in_turn(held, "raw", 6, [P, PACK, BANK], F32)
             rows = src[g * PASS : (g + 1) * PASS, cols]
             nc.sync.dma_start(tile[:], rows.rearrange("(p t) c -> p t c", t=PACK))
             return tile
 
         def weave(planes, width):
-            woven = woven_pool.tile([P, PACK * BANK], BF16, name="woven", align_bytes=64)
+            woven = in_turn(held, "woven", 6, [P, PACK * BANK], BF16)
             nc.scalar.copy(
                 woven[:, : PACK * width].rearrange("p (c i t) -> p c t i", i=4, t=PACK),
                 planes.rearrange("p t (c i) -> p c t i", i=4),
@@ -88,38 +88,57 @@ def tile_list_visa_interview_priority_kernel(
             nc.vector.tensor_copy(picked[:], table.indirect(entries))
             return picked
 
-        wn4_scale_rows = zeroed("wn4_scale_rows", H, U8, nc.vector)
+        wn4_scale_rows = zeroed("wn4_scale_rows", H, U8, nc.gpsimd)
+        identity = keep("identity", [P, P], F32)
+        make_identity(nc, identity[:])
         tab2_scale_rows = zeroed("tab2_scale_rows", TN, U8, nc.vector)
+        tab_scale_rows = zeroed("tab_scale_rows", T, U8, nc.vector)
         idx2 = load_list("idx2", offs2)
         places = load_list("places", pos1)
+        idx = load_list("idx", offs)
+        wgs_rows = keep("wgs_rows", [P, NOTES], F32)
+        nc.sync.dma_start(wgs_rows[:], wgs)
         wn4_raw = keep("wn4_raw", [P, 2 * H], U8)
-        nc.sync.dma_start(wn4_raw[:].bitcast(I32), wn4_words[0].bitcast(I32))
-        load_scale_rows(wn4_scale_rows, wn4_scales)
-        tab2_codes = load_words("tab2_codes", tab2_words[0])
-        load_scale_rows(tab2_scale_rows, tab2_scales)
-        wgs_dealt = keep("wgs_dealt", [P, PACK, NOTES], F32)
-        wgs_rows = wgs.rearrange("(p t) j -> p t j", t=PACK)
-        for planes in (slice(0, 1), slice(1, PACK)):
-            for q in range(4):
-                nc.sync.dma_start(wgs_dealt[32 * q : 32 * q + 32, planes, :], wgs_rows[:, planes, :])
-
+        tab2_codes = keep("tab2_codes", [P, TN], U32)
+        for tile, src in ((wn4_raw, wn4_words[0]), (tab2_codes, tab2_words[0].rearrange("p t i -> p (t i)"))):
+            into, words = tile[:].bitcast(I32), src.bitcast(I32)
+            half = words.shape[1] // 2
+            for cols in (slice(0, half), slice(half, 2 * half)):
+                nc.sync.dma_start(into[:, cols], words[:, cols])
+        load_scale_rows(tab2_scale_rows, tab2_scales, [nc.sync] * 4)
+        load_scale_rows(wn4_scale_rows, wn4_scales, [nc.sync, nc.sync, nc.gpsimd, nc.gpsimd])
         halves = [slice(0, BANK), slice(BANK, 2 * BANK)]
         w1_raw = {(a, 0): load_rows(w1, a, halves[0]) for a in range(2)}
-        idx = load_list("idx", offs)
+        load_scale_rows(tab_scale_rows, tab_scales, [nc.sync] * 4)
+        tab_codes = keep("tab_codes", [P, 2, T], U32)
+        nc.sync.dma_start(tab_codes[:].bitcast(I32), tab_words.rearrange("a p t i -> p a (t i)").bitcast(I32))
 
-        def deal_wn4(g):
-            nc.vector.tensor_copy(
-                wn4_codes[:].bitcast(U16).rearrange("p (t m) -> p t m", t=PACK),
-                wn4_raw[:, 2 * PASS * g : 2 * PASS * (g + 1)].bitcast(U16).rearrange("p (m t) -> p t m", t=PACK),
+        wgs_turned = in_turn(psum, "second", 4, [P, PACK, P], F32)
+        for c in range(PACK):
+            nc.tensor.transpose(wgs_turned[:, c, :], wgs_rows[:, P * c : P * (c + 1)], identity[:])
+        wgs_spread = in_turn(held, "raw", 6, [P, PACK, BANK], F32)
+        wgs_dealt = keep("wgs_dealt", [P, PACK, NOTES], F32)
+        for t in range(PACK):
+            picked_rows = wgs_turned[:].rearrange("j c (m t) -> j c t m", t=PACK)[:, :, t, :]
+            nc.scalar.copy(
+                wgs_spread[:, t, :].rearrange("j (c q m) -> j c q m", c=PACK, q=4),
+                picked_rows.unsqueeze(2).to_broadcast([P, PACK, 4, 32]),
             )
-            nc.vector.tensor_copy(
-                wn4_dealt_scales[:].rearrange("p (t m) -> p t m", t=PACK),
-                wn4_scale_rows[:, PASS * g : PASS * (g + 1)].rearrange("p (m t) -> p t m", t=PACK),
-            )
+            back = in_turn(psum, "second", 4, [P, PACK, P], F32)
+            for c in range(PACK):
+                nc.tensor.transpose(back[:, c, :], wgs_spread[:, t, P * c : P * (c + 1)], identity[:])
+            nc.scalar.copy(wgs_dealt[:, t, :], back[:].rearrange("p c j -> p (c j)"))
 
-        wn4_codes = keep("wn4_codes", [P, 2 * PASS], U8)
-        wn4_dealt_scales = keep("wn4_dealt_scales", [P, PASS], U8)
-        deal_wn4(0)
+        wn4_codes = keep("wn4_codes", [P, 2 * H], U8)
+        nc.vector.tensor_copy(
+            wn4_codes[:].bitcast(U16).rearrange("p (g t m) -> p g t m", g=2, t=PACK),
+            wn4_raw[:].bitcast(U16).rearrange("p (g m t) -> p g t m", g=2, t=PACK),
+        )
+        wn4_dealt_scales = keep("wn4_dealt_scales", [P, H], U8)
+        nc.vector.tensor_copy(
+            wn4_dealt_scales[:].rearrange("p (g t m) -> p g t m", g=2, t=PACK),
+            wn4_scale_rows[:].rearrange("p (g m t) -> p g t m", g=2, t=PACK),
+        )
         v2_codes = keep("v2_codes", [P, NOTES], U32)
         v2_scales = keep("v2_scales", [P, NOTES], U8)
         note_halves = [(slice(256 * u, 256 * (u + 1)), slice(16 * u, 16 * (u + 1))) for u in range(2)]
@@ -128,18 +147,15 @@ def tile_list_visa_interview_priority_kernel(
             nc.vector.tensor_copy(v2_scales[:, cols], tab2_scale_rows[:].indirect(idx2[:, entries]))
 
         pages = [zeroed("page%d" % i, S, F32, nc.vector) for i in range(2)]
-        tab_scale_rows = zeroed("tab_scale_rows", T, U8, nc.gpsimd)
         ws8_scale_rows = zeroed("ws8_scale_rows", N, U8, nc.vector)
-        pages.extend([zeroed("page%d" % i, S, F32, nc.gpsimd) for i in range(2, PAGES)])
+        pages.append(zeroed("page2", S, F32, nc.gpsimd, "tab2_codes"))
+        pages.append(zeroed("page3", S, F32, nc.gpsimd, "tab2_scale_rows"))
 
-        load_scale_rows(tab_scale_rows, tab_scales)
-        tab_codes = keep("tab_codes", [P, 2, T], U32)
-        nc.sync.dma_start(tab_codes[:].bitcast(I32), tab_words.rearrange("a p t i -> p a (t i)").bitcast(I32))
         for a in range(2):
             w1_raw[(a, 1)] = load_rows(w1, a, halves[1])
-        base_rows = {(0, h): load_rows(base, 0, halves[h]) for h in range(2)}
         wz_raw = [load_rows(wz, g, slice(0, N)) for g in range(2)]
-        load_scale_rows(ws8_scale_rows, ws8_scales)
+        base_rows = {(0, h): load_rows(base, 0, halves[h]) for h in range(2)}
+        load_scale_rows(ws8_scale_rows, ws8_scales, [nc.sync] * 4)
         ws8_codes = keep("ws8_codes", [P, 2, N], U32)
         nc.sync.dma_start(
             ws8_codes[:].bitcast(I32), ws8_words.rearrange("a p c i -> p a (c i)").bitcast(I32)
@@ -150,15 +166,13 @@ def tile_list_visa_interview_priority_kernel(
         notes = []
         all_notes = [(slice(0, NOTES), slice(0, NOTES // 16))]
         for s in range(2 * PACK):
-            if s == PACK:
-                deal_wn4(1)
-            strength = row_pool.tile([P, BANK], F32, name="row")
+            strength = in_turn(held, "row", 8, [P, BANK], F32)
             for cols, entries in note_halves if s == 0 else all_notes:
-                acc = first_psum.tile([P, BANK], F32, name="first")
+                acc = in_turn(psum, "first", 4, [P, BANK], F32)
                 nc.tensor.matmul_mx(
                     out=acc[:, cols],
-                    lhsT=wn4_codes[:, 2 * P * (s % PACK) : 2 * P * (s % PACK + 1)].bitcast(E2M1),
-                    lhsT_scale=wn4_dealt_scales[:, P * (s % PACK) : P * (s % PACK + 1)],
+                    lhsT=wn4_codes[:, 2 * P * s : 2 * P * (s + 1)].bitcast(E2M1),
+                    lhsT_scale=wn4_dealt_scales[:, P * s : P * (s + 1)],
                     rhs=v2_codes[:, cols].bitcast(E4M3),
                     rhs_scale=v2_scales[:, cols],
                     start=True,
@@ -166,6 +180,9 @@ def tile_list_visa_interview_priority_kernel(
                 )
                 nc.scalar.activation(strength[:, cols], acc[:, cols], ACT.Abs)
             notes.append(strength)
+
+        pages.append(zeroed("page4", S, F32, nc.gpsimd, "v2_scales"))
+        pages.append(zeroed("page5", S, F32, nc.gpsimd, "v2_codes"))
 
         def place(s):
             for cols, entries in note_halves if s == 0 else all_notes:
@@ -180,7 +197,10 @@ def tile_list_visa_interview_priority_kernel(
             place(s)
 
         def quantise_w1(a, g):
-            woven = woven_pool.tile([P, PACK * BANK], BF16, name="woven", align_bytes=64)
+            if g == 0:
+                woven = keep("w1_woven%d" % a, [P, PACK * BANK], BF16, ("wn4_codes", "wn4_dealt_scales")[a])
+            else:
+                woven = in_turn(held, "woven", 6, [P, PACK * BANK], BF16)
             nc.scalar.copy(
                 woven[:].rearrange("p (t m j) -> p m j t", t=PACK, j=PACK),
                 w1_raw[(a, g)][:].rearrange("p j (m t) -> p m j t", t=PACK),
@@ -197,11 +217,12 @@ def tile_list_visa_interview_priority_kernel(
 
         for a in range(2):
             w1_mx[(a, 1)] = quantise_w1(a, 1)
+        wz_mx = [quantise("wz%d" % g, weave(wz_raw[g][:], N)) for g in range(2)]
 
         def features(g, h):
             a_rows = base_rows[(g, h)]
             for t in range(PACK):
-                acc = first_psum.tile([P, BANK], F32, name="first")
+                acc = in_turn(psum, "first", 4, [P, BANK], F32)
                 cols = slice(P * t, P * (t + 1))
                 for a in range(2):
                     codes, scales = w1_mx[(a, g)]
@@ -220,7 +241,7 @@ def tile_list_visa_interview_priority_kernel(
             h, c0 = divmod(j0, BANK)
             a_rows = base_rows[(g, h)][:, :, c0 : c0 + width]
             a_woven = weave(a_rows, width)
-            z_rows = zrow_pool.tile([P, PACK, BANK], BF16, name="z_rows")
+            z_rows = in_turn(held, "z_rows", 2, [P, PACK, BANK], BF16)
             for t in range(PACK):
                 page = pages[(PACK * g + t) % PAGES]
                 nc.vector.tensor_tensor(
@@ -233,8 +254,8 @@ def tile_list_visa_interview_priority_kernel(
         def second_stage(j0, width, operands):
             per_bank = BANK // width
             for n0 in range(0, N // P, per_bank):
-                skip = second_psum.tile([P, per_bank, width], F32, name="second")
-                y = second_psum.tile([P, per_bank, width], F32, name="second")
+                skip = in_turn(psum, "second", 4, [P, per_bank, width], F32)
+                y = in_turn(psum, "second", 4, [P, per_bank, width], F32)
                 for acc, which in ((skip, 0), (y, 1)):
                     for u in range(per_bank):
                         cols = slice(P * (n0 + u), P * (n0 + u + 1))
@@ -253,9 +274,9 @@ def tile_list_visa_interview_priority_kernel(
                                 start=(g == 0),
                                 stop=(g == 1),
                             )
-                gate = row_pool.tile([P, BANK], F32, name="row")
+                gate = in_turn(held, "row", 8, [P, BANK], F32)
                 nc.scalar.activation(gate[:], skip[:].rearrange("p u j -> p (u j)"), ACT.Tanh)
-                result = row_pool.tile([P, BANK], F32, name="row")
+                result = in_turn(held, "row", 8, [P, BANK], F32)
                 nc.vector.tensor_tensor(result[:], y[:].rearrange("p u j -> p (u j)"), gate[:], ALU.mult)
                 rows = out[P * n0 : P * (n0 + per_bank), j0 : j0 + width]
                 nc.sync.dma_start(
@@ -268,7 +289,6 @@ def tile_list_visa_interview_priority_kernel(
             first_pass.append(quantise_a_z(0, BANK * h, BANK))
         for s in range(PAGES, 2 * PACK):
             place(s)
-        wz_mx = [quantise("wz%d" % g, weave(wz_raw[g][:], N)) for g in range(2)]
 
         for j0, width in ((0, 512), (512, 256), (768, 256)):
             h, c0 = divmod(j0, BANK)

@@ -21,7 +21,16 @@ P = 128
 PACK = 4
 PASS = P * PACK
 BANK = 512
+QUADRANTS = 4
+PER_COLUMN = 16
+SLICES = H // P
 PAGES = 6
+RAW_SLOTS = 6
+WOVEN_SLOTS = 6
+ROW_SLOTS = SLICES
+Z_SLOTS = 2
+BANKS_A_STAGE = 4
+PIECES = ((0, 512), (512, 256), (768, 256))
 
 
 def tile_list_visa_interview_priority_kernel(
@@ -34,21 +43,27 @@ def tile_list_visa_interview_priority_kernel(
         psum = ctx.enter_context(tc.psum_pool(name="psum", bufs=1))
         turns = {}
 
-        def in_turn(pool, ring, slots, shape, dtype):
-            turn = turns.get(ring, 0)
-            turns[ring] = turn + 1
-            name = "%s%d" % (ring, turn % slots)
-            if pool is psum:
-                return pool.tile(shape, dtype, name=name, tag=name)
-            return pool.tile(shape, dtype, name=name, tag=name, align_bytes=64)
-
         def keep(name, shape, dtype, slot=""):
             return held.tile(shape, dtype, name=name, tag=slot or name, align_bytes=64)
 
+        def next_slot(ring, slots):
+            turn = turns.get(ring, 0)
+            turns[ring] = turn + 1
+            return "%s%d" % (ring, turn % slots)
+
+        def bank(stage, shape):
+            name = next_slot(stage, BANKS_A_STAGE)
+            return psum.tile(shape, F32, name=name, tag=name)
+
+        def row_tile():
+            return keep(next_slot("row", ROW_SLOTS), [P, BANK], F32)
+
+        def woven_tile():
+            return keep(next_slot("woven", WOVEN_SLOTS), [P, PACK * BANK], BF16)
+
         def zeroed(name, width, dtype, engine, slot=""):
             tile = keep(name, [P, width], dtype, slot)
-            view = tile[:].bitcast(I32) if dtype == U8 else tile[:]
-            engine.memset(view, 0)
+            engine.memset(tile[:].bitcast(I32) if dtype == U8 else tile[:], 0)
             return tile
 
         def load_list(name, src):
@@ -58,23 +73,23 @@ def tile_list_visa_interview_priority_kernel(
 
         def load_scale_rows(tile, src, queues):
             passes = src.shape[0]
-            for q in range(4):
+            for q in range(QUADRANTS):
                 rows = src[:, 4 * q : 4 * q + 4, :] if passes > 1 else src[0, 4 * q : 4 * q + 4, :]
                 queues[q].dma_start(tile[32 * q : 32 * q + 4 * passes, :].bitcast(I32), rows.bitcast(I32))
 
         def load_rows(src, g, cols):
-            tile = in_turn(held, "raw", 6, [P, PACK, BANK], F32)
+            tile = keep(next_slot("raw", RAW_SLOTS), [P, PACK, BANK], F32)
             rows = src[g * PASS : (g + 1) * PASS, cols]
             nc.sync.dma_start(tile[:], rows.rearrange("(p t) c -> p t c", t=PACK))
             return tile
 
-        def weave(planes, width):
-            woven = in_turn(held, "woven", 6, [P, PACK * BANK], BF16)
-            nc.scalar.copy(
-                woven[:, : PACK * width].rearrange("p (c i t) -> p c t i", i=4, t=PACK),
+        def weave(planes, copy):
+            woven = woven_tile()[:, : PACK * planes.shape[2]]
+            copy(
+                woven.rearrange("p (c i t) -> p c t i", i=4, t=PACK),
                 planes.rearrange("p t (c i) -> p c t i", i=4),
             )
-            return woven[:, : PACK * width]
+            return woven
 
         def quantise(name, woven):
             width = woven.shape[1] // PACK
@@ -83,10 +98,20 @@ def tile_list_visa_interview_priority_kernel(
             nc.vector.quantize_mx(out=codes[:].bitcast(E4M3), scales=scales[:], in_=woven)
             return codes, scales
 
-        def gather(name, table, entries, dtype):
-            picked = keep(name, [P, 16 * entries.shape[1]], dtype)
-            nc.vector.tensor_copy(picked[:], table.indirect(entries))
-            return picked
+        def multiply(acc, passes):
+            for number, (w_codes, w_scales, x_codes, x_scales) in enumerate(passes):
+                nc.tensor.matmul_mx(
+                    out=acc,
+                    lhsT=w_codes,
+                    lhsT_scale=w_scales,
+                    rhs=x_codes.bitcast(E4M3),
+                    rhs_scale=x_scales,
+                    start=(number == 0),
+                    stop=(number == len(passes) - 1),
+                )
+
+        def list_columns(entries):
+            return slice(entries.start // PER_COLUMN, entries.stop // PER_COLUMN)
 
         wn4_scale_rows = zeroed("wn4_scale_rows", H, U8, nc.gpsimd)
         identity = keep("identity", [P, P], F32)
@@ -102,30 +127,30 @@ def tile_list_visa_interview_priority_kernel(
         tab2_codes = keep("tab2_codes", [P, TN], U32)
         for tile, src in ((wn4_raw, wn4_words[0]), (tab2_codes, tab2_words[0].rearrange("p t i -> p (t i)"))):
             into, words = tile[:].bitcast(I32), src.bitcast(I32)
-            half = words.shape[1] // 2
-            for cols in (slice(0, half), slice(half, 2 * half)):
+            middle = words.shape[1] // 2
+            for cols in (slice(0, middle), slice(middle, 2 * middle)):
                 nc.sync.dma_start(into[:, cols], words[:, cols])
-        load_scale_rows(tab2_scale_rows, tab2_scales, [nc.sync] * 4)
+        load_scale_rows(tab2_scale_rows, tab2_scales, [nc.sync] * QUADRANTS)
         load_scale_rows(wn4_scale_rows, wn4_scales, [nc.sync, nc.sync, nc.gpsimd, nc.gpsimd])
         halves = [slice(0, BANK), slice(BANK, 2 * BANK)]
         w1_raw = {(a, 0): load_rows(w1, a, halves[0]) for a in range(2)}
-        load_scale_rows(tab_scale_rows, tab_scales, [nc.sync] * 4)
+        load_scale_rows(tab_scale_rows, tab_scales, [nc.sync] * QUADRANTS)
         tab_codes = keep("tab_codes", [P, 2, T], U32)
         nc.sync.dma_start(tab_codes[:].bitcast(I32), tab_words.rearrange("a p t i -> p a (t i)").bitcast(I32))
 
-        wgs_turned = in_turn(psum, "second", 4, [P, PACK, P], F32)
-        for c in range(PACK):
+        wgs_turned = bank("second", [P, PACK, P])
+        for c in range(NOTES // P):
             nc.tensor.transpose(wgs_turned[:, c, :], wgs_rows[:, P * c : P * (c + 1)], identity[:])
-        wgs_spread = in_turn(held, "raw", 6, [P, PACK, BANK], F32)
+        wgs_spread = keep(next_slot("raw", RAW_SLOTS), [P, PACK, BANK], F32)
         wgs_dealt = keep("wgs_dealt", [P, PACK, NOTES], F32)
         for t in range(PACK):
             picked_rows = wgs_turned[:].rearrange("j c (m t) -> j c t m", t=PACK)[:, :, t, :]
             nc.scalar.copy(
-                wgs_spread[:, t, :].rearrange("j (c q m) -> j c q m", c=PACK, q=4),
-                picked_rows.unsqueeze(2).to_broadcast([P, PACK, 4, 32]),
+                wgs_spread[:, t, :].rearrange("j (c q m) -> j c q m", c=NOTES // P, q=QUADRANTS),
+                picked_rows.unsqueeze(2).to_broadcast([P, NOTES // P, QUADRANTS, 32]),
             )
-            back = in_turn(psum, "second", 4, [P, PACK, P], F32)
-            for c in range(PACK):
+            back = bank("second", [P, PACK, P])
+            for c in range(NOTES // P):
                 nc.tensor.transpose(back[:, c, :], wgs_spread[:, t, P * c : P * (c + 1)], identity[:])
             nc.scalar.copy(wgs_dealt[:, t, :], back[:].rearrange("p c j -> p (c j)"))
 
@@ -141,10 +166,13 @@ def tile_list_visa_interview_priority_kernel(
         )
         v2_codes = keep("v2_codes", [P, NOTES], U32)
         v2_scales = keep("v2_scales", [P, NOTES], U8)
-        note_halves = [(slice(256 * u, 256 * (u + 1)), slice(16 * u, 16 * (u + 1))) for u in range(2)]
-        for cols, entries in note_halves:
-            nc.vector.tensor_copy(v2_codes[:, cols], tab2_codes[:].indirect(idx2[:, entries]))
-            nc.vector.tensor_copy(v2_scales[:, cols], tab2_scale_rows[:].indirect(idx2[:, entries]))
+        note_halves = [slice(0, NOTES // 2), slice(NOTES // 2, NOTES)]
+        for part in note_halves:
+            nc.vector.tensor_copy(v2_codes[:, part], tab2_codes[:].indirect(idx2[:, list_columns(part)]))
+            nc.vector.tensor_copy(v2_scales[:, part], tab2_scale_rows[:].indirect(idx2[:, list_columns(part)]))
+
+        def note_parts(s):
+            return note_halves if s == 0 else [slice(0, NOTES)]
 
         pages = [zeroed("page%d" % i, S, F32, nc.vector) for i in range(2)]
         ws8_scale_rows = zeroed("ws8_scale_rows", N, U8, nc.vector)
@@ -154,150 +182,130 @@ def tile_list_visa_interview_priority_kernel(
         for a in range(2):
             w1_raw[(a, 1)] = load_rows(w1, a, halves[1])
         wz_raw = [load_rows(wz, g, slice(0, N)) for g in range(2)]
-        base_rows = {(0, h): load_rows(base, 0, halves[h]) for h in range(2)}
-        load_scale_rows(ws8_scale_rows, ws8_scales, [nc.sync] * 4)
+        a_rows = {(0, h): load_rows(base, 0, halves[h]) for h in range(2)}
+        load_scale_rows(ws8_scale_rows, ws8_scales, [nc.sync] * QUADRANTS)
         ws8_codes = keep("ws8_codes", [P, 2, N], U32)
-        nc.sync.dma_start(
-            ws8_codes[:].bitcast(I32), ws8_words.rearrange("a p c i -> p a (c i)").bitcast(I32)
-        )
+        nc.sync.dma_start(ws8_codes[:].bitcast(I32), ws8_words.rearrange("a p c i -> p a (c i)").bitcast(I32))
         for h in range(2):
-            base_rows[(1, h)] = load_rows(base, 1, halves[h])
+            a_rows[(1, h)] = load_rows(base, 1, halves[h])
 
-        notes = []
-        all_notes = [(slice(0, NOTES), slice(0, NOTES // 16))]
-        for s in range(2 * PACK):
-            strength = in_turn(held, "row", 8, [P, BANK], F32)
-            for cols, entries in note_halves if s == 0 else all_notes:
-                acc = in_turn(psum, "first", 4, [P, BANK], F32)
-                nc.tensor.matmul_mx(
-                    out=acc[:, cols],
-                    lhsT=wn4_codes[:, 2 * P * s : 2 * P * (s + 1)].bitcast(E2M1),
-                    lhsT_scale=wn4_dealt_scales[:, P * s : P * (s + 1)],
-                    rhs=v2_codes[:, cols].bitcast(E4M3),
-                    rhs_scale=v2_scales[:, cols],
-                    start=True,
-                    stop=True,
-                )
-                nc.scalar.activation(strength[:, cols], acc[:, cols], ACT.Abs)
-            notes.append(strength)
+        strengths = []
+        for s in range(SLICES):
+            strength = row_tile()
+            for part in note_parts(s):
+                acc = bank("first", [P, BANK])
+                multiply(acc[:, part], [(
+                    wn4_codes[:, 2 * P * s : 2 * P * (s + 1)].bitcast(E2M1),
+                    wn4_dealt_scales[:, P * s : P * (s + 1)],
+                    v2_codes[:, part],
+                    v2_scales[:, part],
+                )])
+                nc.scalar.activation(strength[:, part], acc[:, part], ACT.Abs)
+            strengths.append(strength)
 
         pages.append(zeroed("page4", S, F32, nc.gpsimd, "v2_scales"))
         pages.append(zeroed("page5", S, F32, nc.gpsimd, "v2_codes"))
 
         def place(s):
-            for cols, entries in note_halves if s == 0 else all_notes:
+            for part in note_parts(s):
                 nc.vector.tensor_tensor(
-                    pages[s % PAGES][:].indirect(places[:, entries]),
-                    notes[s][:, cols],
-                    wgs_dealt[:, s % PACK, cols],
+                    pages[s % PAGES][:].indirect(places[:, list_columns(part)]),
+                    strengths[s][:, part],
+                    wgs_dealt[:, s % PACK, part],
                     ALU.mult,
                 )
 
         for s in range(PAGES):
             place(s)
 
-        def quantise_w1(a, g):
-            if g == 0:
-                woven = keep("w1_woven%d" % a, [P, PACK * BANK], BF16, ("wn4_codes", "wn4_dealt_scales")[a])
-            else:
-                woven = in_turn(held, "woven", 6, [P, PACK * BANK], BF16)
+        def quantise_w1(a, g, woven):
             nc.scalar.copy(
-                woven[:].rearrange("p (t m j) -> p m j t", t=PACK, j=PACK),
-                w1_raw[(a, g)][:].rearrange("p j (m t) -> p m j t", t=PACK),
+                woven[:].rearrange("p (t m i) -> p m i t", t=PACK, i=PACK),
+                w1_raw[(a, g)][:].rearrange("p i (m t) -> p m i t", t=PACK),
             )
             return quantise("w1_%d_%d" % (a, g), woven[:])
 
-        w1_mx = {(a, 0): quantise_w1(a, 0) for a in range(2)}
+        def gather(name, window, entries, dtype):
+            picked = keep(name, [P, BANK], dtype)
+            nc.vector.tensor_copy(picked[:], window.indirect(idx[:, list_columns(entries)]))
+            return picked
+
+        w1_mx = {}
+        for a, slot in enumerate(("wn4_codes", "wn4_dealt_scales")):
+            w1_mx[(a, 0)] = quantise_w1(a, 0, keep("w1_woven%d" % a, [P, PACK * BANK], BF16, slot))
         v_codes, v_scales = {}, {}
         for h in range(2):
-            entries = idx[:, 32 * h : 32 * (h + 1)]
-            v_scales[h] = gather("v_scales%d" % h, tab_scale_rows[:], entries, U8)
+            v_scales[h] = gather("v_scales%d" % h, tab_scale_rows[:], halves[h], U8)
             for a in range(2):
-                v_codes[(a, h)] = gather("v_codes%d_%d" % (a, h), tab_codes[:, a, :], entries, U32)
-
+                v_codes[(a, h)] = gather("v_codes%d_%d" % (a, h), tab_codes[:, a, :], halves[h], U32)
         for a in range(2):
-            w1_mx[(a, 1)] = quantise_w1(a, 1)
-        wz_mx = [quantise("wz%d" % g, weave(wz_raw[g][:], N)) for g in range(2)]
+            w1_mx[(a, 1)] = quantise_w1(a, 1, woven_tile())
+        wz_mx = [quantise("wz%d" % g, weave(wz_raw[g][:], nc.scalar.copy)) for g in range(2)]
 
         def features(g, h):
-            a_rows = base_rows[(g, h)]
             for t in range(PACK):
-                acc = in_turn(psum, "first", 4, [P, BANK], F32)
+                acc = bank("first", [P, BANK])
                 cols = slice(P * t, P * (t + 1))
-                for a in range(2):
-                    codes, scales = w1_mx[(a, g)]
-                    nc.tensor.matmul_mx(
-                        out=acc[:],
-                        lhsT=codes[:, cols].bitcast(E4M3),
-                        lhsT_scale=scales[:, cols],
-                        rhs=v_codes[(a, h)][:].bitcast(E4M3),
-                        rhs_scale=v_scales[h][4 * a :, :],
-                        start=(a == 0),
-                        stop=(a == 1),
-                    )
-                nc.vector.tensor_tensor(a_rows[:, t, :], acc[:], a_rows[:, t, :], ALU.subtract)
+                multiply(acc[:], [
+                    (w1_mx[(a, g)][0][:, cols].bitcast(E4M3), w1_mx[(a, g)][1][:, cols],
+                     v_codes[(a, h)][:], v_scales[h][4 * a :, :])
+                    for a in range(2)
+                ])
+                rows = a_rows[(g, h)][:, t, :]
+                nc.vector.tensor_tensor(rows, acc[:], rows, ALU.subtract)
 
-        def quantise_a_z(g, j0, width):
+        def quantise_a_z(g, j0, width, z_copy):
             h, c0 = divmod(j0, BANK)
-            a_rows = base_rows[(g, h)][:, :, c0 : c0 + width]
-            a_woven = weave(a_rows, width)
-            z_rows = in_turn(held, "z_rows", 2, [P, PACK, BANK], BF16)
+            a_piece = a_rows[(g, h)][:, :, c0 : c0 + width]
+            a_woven = weave(a_piece, nc.scalar.copy)
+            z_rows = keep(next_slot("z_rows", Z_SLOTS), [P, PACK, BANK], BF16)
             for t in range(PACK):
                 page = pages[(PACK * g + t) % PAGES]
-                nc.vector.tensor_tensor(
-                    z_rows[:, t, :width], a_rows[:, t, :], page[:, j0 : j0 + width], ALU.max
-                )
-            z_woven = weave(z_rows[:, :, :width], width)
-            tag = "%d_%d" % (g, j0)
-            return quantise("a" + tag, a_woven), quantise("z" + tag, z_woven)
+                nc.vector.tensor_tensor(z_rows[:, t, :width], a_piece[:, t, :], page[:, j0 : j0 + width], ALU.max)
+            z_woven = weave(z_rows[:, :, :width], z_copy)
+            piece = "%d_%d" % (g, j0)
+            return quantise("a" + piece, a_woven), quantise("z" + piece, z_woven)
 
-        def second_stage(j0, width, operands):
-            per_bank = BANK // width
-            for n0 in range(0, N // P, per_bank):
-                skip = in_turn(psum, "second", 4, [P, per_bank, width], F32)
-                y = in_turn(psum, "second", 4, [P, per_bank, width], F32)
-                for acc, which in ((skip, 0), (y, 1)):
-                    for u in range(per_bank):
-                        cols = slice(P * (n0 + u), P * (n0 + u + 1))
-                        for g in range(2):
-                            codes, scales = operands[g][which]
-                            if which == 0:
-                                w_codes, w_scales = ws8_codes[:, g, cols], ws8_scale_rows[4 * g :, cols]
-                            else:
-                                w_codes, w_scales = wz_mx[g][0][:, cols], wz_mx[g][1][:, cols]
-                            nc.tensor.matmul_mx(
-                                out=acc[:, u, :],
-                                lhsT=w_codes.bitcast(E4M3),
-                                lhsT_scale=w_scales,
-                                rhs=codes.bitcast(E4M3),
-                                rhs_scale=scales,
-                                start=(g == 0),
-                                stop=(g == 1),
-                            )
-                gate = in_turn(held, "row", 8, [P, BANK], F32)
+        def second_stage(j0, width, a_mx, z_mx, skip_banks):
+            groups = BANK // width
+            for n0 in range(0, N // P, groups):
+                skip = bank(skip_banks, [P, groups, width])
+                y = bank("second", [P, groups, width])
+                columns = [slice(P * (n0 + u), P * (n0 + u + 1)) for u in range(groups)]
+                for u, cols in enumerate(columns):
+                    multiply(skip[:, u, :], [
+                        (ws8_codes[:, g, cols].bitcast(E4M3), ws8_scale_rows[4 * g :, cols]) + a_mx[g]
+                        for g in range(2)
+                    ])
+                for u, cols in enumerate(columns):
+                    multiply(y[:, u, :], [
+                        (wz_mx[g][0][:, cols].bitcast(E4M3), wz_mx[g][1][:, cols]) + z_mx[g] for g in range(2)
+                    ])
+                gate = row_tile()
                 nc.scalar.activation(gate[:], skip[:].rearrange("p u j -> p (u j)"), ACT.Tanh)
-                result = in_turn(held, "row", 8, [P, BANK], F32)
+                result = row_tile()
                 nc.vector.tensor_tensor(result[:], y[:].rearrange("p u j -> p (u j)"), gate[:], ALU.mult)
-                rows = out[P * n0 : P * (n0 + per_bank), j0 : j0 + width]
+                rows = out[P * n0 : P * (n0 + groups), j0 : j0 + width]
                 nc.sync.dma_start(
-                    rows.rearrange("(u p) j -> p u j", p=P), result[:].rearrange("p (u j) -> p u j", u=per_bank)
+                    rows.rearrange("(u p) j -> p u j", p=P), result[:].rearrange("p (u j) -> p u j", u=groups)
                 )
 
-        first_pass = []
+        first_half = []
         for h in range(2):
             features(0, h)
-            first_pass.append(quantise_a_z(0, BANK * h, BANK))
-        for s in range(PAGES, 2 * PACK):
+            first_half.append(quantise_a_z(0, BANK * h, BANK, nc.scalar.copy))
+        for s in range(PAGES, SLICES):
             place(s)
 
-        for j0, width in ((0, 512), (512, 256), (768, 256)):
+        for j0, width in PIECES:
             h, c0 = divmod(j0, BANK)
             if c0 == 0:
                 features(1, h)
-            last = quantise_a_z(1, j0, width)
+            z_copy = nc.vector.tensor_copy if j0 + width == S else nc.scalar.copy
+            second_half = quantise_a_z(1, j0, width, z_copy)
             cols = slice(c0, c0 + width)
-            operands = [
-                [(codes[:, cols], scales[:, cols]) for codes, scales in first_pass[h]],
-                [(codes[:], scales[:]) for codes, scales in last],
+            a_mx, z_mx = [
+                [(first[0][:, cols], first[1][:, cols]), (second[0][:], second[1][:])]
+                for first, second in zip(first_half[h], second_half)
             ]
-            second_stage(j0, width, operands)
+            second_stage(j0, width, a_mx, z_mx, "first" if h == 1 else "second")

from contextlib import ExitStack

import concourse.mybir as mybir
from concourse.masks import make_identity

K, KN, H, N, T, TN, S, NOTES = 1024, 512, 1024, 512, 4096, 2048, 1024, 512
FLOPS = 2 * (K * H * S + KN * H * NOTES + 2 * H * N * S)

F32 = mybir.dt.float32
BF16 = mybir.dt.bfloat16
I32 = mybir.dt.int32
U32 = mybir.dt.uint32
U16 = mybir.dt.uint16
U8 = mybir.dt.uint8
E4M3 = mybir.dt.float8_e4m3fn_x4
E2M1 = mybir.dt.float4_e2m1fn_x4
ALU = mybir.AluOpType
ACT = mybir.ActivationFunctionType

P = 128
PACK = 4
PASS = P * PACK
BANK = 512
QUADRANTS = 4
PER_COLUMN = 16
SLICES = H // P
PAGES = 6
RAW_SLOTS = 6
WOVEN_SLOTS = 6
ROW_SLOTS = SLICES
Z_SLOTS = 2
BANKS_A_STAGE = 4
PIECES = ((0, 512), (512, 256), (768, 256))


def tile_list_visa_interview_priority_kernel(
    tc, tab_words, tab_scales, tab2_words, tab2_scales, offs, offs2, pos1, w1, base,
    wn4_words, wn4_scales, wgs, wz, ws8_words, ws8_scales, out,
):
    nc = tc.nc
    with ExitStack() as ctx:
        held = ctx.enter_context(tc.tile_pool(name="held", bufs=1))
        psum = ctx.enter_context(tc.psum_pool(name="psum", bufs=1))
        turns = {}

        def keep(name, shape, dtype, slot=""):
            return held.tile(shape, dtype, name=name, tag=slot or name, align_bytes=64)

        def next_slot(ring, slots):
            turn = turns.get(ring, 0)
            turns[ring] = turn + 1
            return "%s%d" % (ring, turn % slots)

        def bank(stage, shape):
            name = next_slot(stage, BANKS_A_STAGE)
            return psum.tile(shape, F32, name=name, tag=name)

        def row_tile():
            return keep(next_slot("row", ROW_SLOTS), [P, BANK], F32)

        def woven_tile():
            return keep(next_slot("woven", WOVEN_SLOTS), [P, PACK * BANK], BF16)

        def zeroed(name, width, dtype, engine, slot=""):
            tile = keep(name, [P, width], dtype, slot)
            engine.memset(tile[:].bitcast(I32) if dtype == U8 else tile[:], 0)
            return tile

        def load_list(name, src):
            tile = held.tile(list(src.shape), U16, name=name)
            nc.sync.dma_start(tile[:], src)
            return tile

        def load_scale_rows(tile, src, queues):
            passes = src.shape[0]
            for q in range(QUADRANTS):
                rows = src[:, 4 * q : 4 * q + 4, :] if passes > 1 else src[0, 4 * q : 4 * q + 4, :]
                queues[q].dma_start(tile[32 * q : 32 * q + 4 * passes, :].bitcast(I32), rows.bitcast(I32))

        def load_rows(src, g, cols):
            tile = keep(next_slot("raw", RAW_SLOTS), [P, PACK, BANK], F32)
            rows = src[g * PASS : (g + 1) * PASS, cols]
            nc.sync.dma_start(tile[:], rows.rearrange("(p t) c -> p t c", t=PACK))
            return tile

        def weave(planes, copy):
            woven = woven_tile()[:, : PACK * planes.shape[2]]
            copy(
                woven.rearrange("p (c i t) -> p c t i", i=4, t=PACK),
                planes.rearrange("p t (c i) -> p c t i", i=4),
            )
            return woven

        def quantise(name, woven):
            width = woven.shape[1] // PACK
            codes = keep(name + "_codes", [P, width], U32)
            scales = keep(name + "_scales", [P, width], U8)
            nc.vector.quantize_mx(out=codes[:].bitcast(E4M3), scales=scales[:], in_=woven)
            return codes, scales

        def multiply(acc, passes):
            for number, (w_codes, w_scales, x_codes, x_scales) in enumerate(passes):
                nc.tensor.matmul_mx(
                    out=acc,
                    lhsT=w_codes,
                    lhsT_scale=w_scales,
                    rhs=x_codes.bitcast(E4M3),
                    rhs_scale=x_scales,
                    start=(number == 0),
                    stop=(number == len(passes) - 1),
                )

        def list_columns(entries):
            return slice(entries.start // PER_COLUMN, entries.stop // PER_COLUMN)

        wn4_scale_rows = zeroed("wn4_scale_rows", H, U8, nc.gpsimd)
        identity = keep("identity", [P, P], F32)
        make_identity(nc, identity[:])
        tab2_scale_rows = zeroed("tab2_scale_rows", TN, U8, nc.vector)
        tab_scale_rows = zeroed("tab_scale_rows", T, U8, nc.vector)
        idx2 = load_list("idx2", offs2)
        places = load_list("places", pos1)
        idx = load_list("idx", offs)
        wgs_rows = keep("wgs_rows", [P, NOTES], F32)
        nc.sync.dma_start(wgs_rows[:], wgs)
        wn4_raw = keep("wn4_raw", [P, 2 * H], U8)
        tab2_codes = keep("tab2_codes", [P, TN], U32)
        for tile, src in ((wn4_raw, wn4_words[0]), (tab2_codes, tab2_words[0].rearrange("p t i -> p (t i)"))):
            into, words = tile[:].bitcast(I32), src.bitcast(I32)
            middle = words.shape[1] // 2
            for cols in (slice(0, middle), slice(middle, 2 * middle)):
                nc.sync.dma_start(into[:, cols], words[:, cols])
        load_scale_rows(tab2_scale_rows, tab2_scales, [nc.sync] * QUADRANTS)
        load_scale_rows(wn4_scale_rows, wn4_scales, [nc.sync, nc.sync, nc.gpsimd, nc.gpsimd])
        halves = [slice(0, BANK), slice(BANK, 2 * BANK)]
        w1_raw = {(a, 0): load_rows(w1, a, halves[0]) for a in range(2)}
        load_scale_rows(tab_scale_rows, tab_scales, [nc.sync] * QUADRANTS)
        tab_codes = keep("tab_codes", [P, 2, T], U32)
        nc.sync.dma_start(tab_codes[:].bitcast(I32), tab_words.rearrange("a p t i -> p a (t i)").bitcast(I32))

        wgs_turned = bank("second", [P, PACK, P])
        for c in range(NOTES // P):
            nc.tensor.transpose(wgs_turned[:, c, :], wgs_rows[:, P * c : P * (c + 1)], identity[:])
        wgs_spread = keep(next_slot("raw", RAW_SLOTS), [P, PACK, BANK], F32)
        wgs_dealt = keep("wgs_dealt", [P, PACK, NOTES], F32)
        for t in range(PACK):
            picked_rows = wgs_turned[:].rearrange("j c (m t) -> j c t m", t=PACK)[:, :, t, :]
            nc.scalar.copy(
                wgs_spread[:, t, :].rearrange("j (c q m) -> j c q m", c=NOTES // P, q=QUADRANTS),
                picked_rows.unsqueeze(2).to_broadcast([P, NOTES // P, QUADRANTS, 32]),
            )
            back = bank("second", [P, PACK, P])
            for c in range(NOTES // P):
                nc.tensor.transpose(back[:, c, :], wgs_spread[:, t, P * c : P * (c + 1)], identity[:])
            nc.scalar.copy(wgs_dealt[:, t, :], back[:].rearrange("p c j -> p (c j)"))

        wn4_codes = keep("wn4_codes", [P, 2 * H], U8)
        nc.vector.tensor_copy(
            wn4_codes[:].bitcast(U16).rearrange("p (g t m) -> p g t m", g=2, t=PACK),
            wn4_raw[:].bitcast(U16).rearrange("p (g m t) -> p g t m", g=2, t=PACK),
        )
        wn4_dealt_scales = keep("wn4_dealt_scales", [P, H], U8)
        nc.vector.tensor_copy(
            wn4_dealt_scales[:].rearrange("p (g t m) -> p g t m", g=2, t=PACK),
            wn4_scale_rows[:].rearrange("p (g m t) -> p g t m", g=2, t=PACK),
        )
        v2_codes = keep("v2_codes", [P, NOTES], U32)
        v2_scales = keep("v2_scales", [P, NOTES], U8)
        note_halves = [slice(0, NOTES // 2), slice(NOTES // 2, NOTES)]
        for part in note_halves:
            nc.vector.tensor_copy(v2_codes[:, part], tab2_codes[:].indirect(idx2[:, list_columns(part)]))
            nc.vector.tensor_copy(v2_scales[:, part], tab2_scale_rows[:].indirect(idx2[:, list_columns(part)]))

        def note_parts(s):
            return note_halves if s == 0 else [slice(0, NOTES)]

        pages = [zeroed("page%d" % i, S, F32, nc.vector) for i in range(2)]
        ws8_scale_rows = zeroed("ws8_scale_rows", N, U8, nc.vector)
        pages.append(zeroed("page2", S, F32, nc.gpsimd, "tab2_codes"))
        pages.append(zeroed("page3", S, F32, nc.gpsimd, "tab2_scale_rows"))

        for a in range(2):
            w1_raw[(a, 1)] = load_rows(w1, a, halves[1])
        wz_raw = [load_rows(wz, g, slice(0, N)) for g in range(2)]
        a_rows = {(0, h): load_rows(base, 0, halves[h]) for h in range(2)}
        load_scale_rows(ws8_scale_rows, ws8_scales, [nc.sync] * QUADRANTS)
        ws8_codes = keep("ws8_codes", [P, 2, N], U32)
        nc.sync.dma_start(ws8_codes[:].bitcast(I32), ws8_words.rearrange("a p c i -> p a (c i)").bitcast(I32))
        for h in range(2):
            a_rows[(1, h)] = load_rows(base, 1, halves[h])

        strengths = []
        for s in range(SLICES):
            strength = row_tile()
            for part in note_parts(s):
                acc = bank("first", [P, BANK])
                multiply(acc[:, part], [(
                    wn4_codes[:, 2 * P * s : 2 * P * (s + 1)].bitcast(E2M1),
                    wn4_dealt_scales[:, P * s : P * (s + 1)],
                    v2_codes[:, part],
                    v2_scales[:, part],
                )])
                nc.scalar.activation(strength[:, part], acc[:, part], ACT.Abs)
            strengths.append(strength)

        pages.append(zeroed("page4", S, F32, nc.gpsimd, "v2_scales"))
        pages.append(zeroed("page5", S, F32, nc.gpsimd, "v2_codes"))

        def place(s):
            for part in note_parts(s):
                nc.vector.tensor_tensor(
                    pages[s % PAGES][:].indirect(places[:, list_columns(part)]),
                    strengths[s][:, part],
                    wgs_dealt[:, s % PACK, part],
                    ALU.mult,
                )

        for s in range(PAGES):
            place(s)

        def quantise_w1(a, g, woven):
            nc.scalar.copy(
                woven[:].rearrange("p (t m i) -> p m i t", t=PACK, i=PACK),
                w1_raw[(a, g)][:].rearrange("p i (m t) -> p m i t", t=PACK),
            )
            return quantise("w1_%d_%d" % (a, g), woven[:])

        def gather(name, window, entries, dtype):
            picked = keep(name, [P, BANK], dtype)
            nc.vector.tensor_copy(picked[:], window.indirect(idx[:, list_columns(entries)]))
            return picked

        w1_mx = {}
        for a, slot in enumerate(("wn4_codes", "wn4_dealt_scales")):
            w1_mx[(a, 0)] = quantise_w1(a, 0, keep("w1_woven%d" % a, [P, PACK * BANK], BF16, slot))
        v_codes, v_scales = {}, {}
        for h in range(2):
            v_scales[h] = gather("v_scales%d" % h, tab_scale_rows[:], halves[h], U8)
            for a in range(2):
                v_codes[(a, h)] = gather("v_codes%d_%d" % (a, h), tab_codes[:, a, :], halves[h], U32)
        for a in range(2):
            w1_mx[(a, 1)] = quantise_w1(a, 1, woven_tile())
        wz_mx = [quantise("wz%d" % g, weave(wz_raw[g][:], nc.scalar.copy)) for g in range(2)]

        def features(g, h):
            for t in range(PACK):
                acc = bank("first", [P, BANK])
                cols = slice(P * t, P * (t + 1))
                multiply(acc[:], [
                    (w1_mx[(a, g)][0][:, cols].bitcast(E4M3), w1_mx[(a, g)][1][:, cols],
                     v_codes[(a, h)][:], v_scales[h][4 * a :, :])
                    for a in range(2)
                ])
                rows = a_rows[(g, h)][:, t, :]
                nc.vector.tensor_tensor(rows, acc[:], rows, ALU.subtract)

        def quantise_a_z(g, j0, width, z_copy):
            h, c0 = divmod(j0, BANK)
            a_piece = a_rows[(g, h)][:, :, c0 : c0 + width]
            a_woven = weave(a_piece, nc.scalar.copy)
            z_rows = keep(next_slot("z_rows", Z_SLOTS), [P, PACK, BANK], BF16)
            for t in range(PACK):
                page = pages[(PACK * g + t) % PAGES]
                nc.vector.tensor_tensor(z_rows[:, t, :width], a_piece[:, t, :], page[:, j0 : j0 + width], ALU.max)
            z_woven = weave(z_rows[:, :, :width], z_copy)
            piece = "%d_%d" % (g, j0)
            return quantise("a" + piece, a_woven), quantise("z" + piece, z_woven)

        def second_stage(j0, width, a_mx, z_mx, skip_banks):
            groups = BANK // width
            for n0 in range(0, N // P, groups):
                skip = bank(skip_banks, [P, groups, width])
                y = bank("second", [P, groups, width])
                columns = [slice(P * (n0 + u), P * (n0 + u + 1)) for u in range(groups)]
                for u, cols in enumerate(columns):
                    multiply(skip[:, u, :], [
                        (ws8_codes[:, g, cols].bitcast(E4M3), ws8_scale_rows[4 * g :, cols]) + a_mx[g]
                        for g in range(2)
                    ])
                for u, cols in enumerate(columns):
                    multiply(y[:, u, :], [
                        (wz_mx[g][0][:, cols].bitcast(E4M3), wz_mx[g][1][:, cols]) + z_mx[g] for g in range(2)
                    ])
                gate = row_tile()
                nc.scalar.activation(gate[:], skip[:].rearrange("p u j -> p (u j)"), ACT.Tanh)
                result = row_tile()
                nc.vector.tensor_tensor(result[:], y[:].rearrange("p u j -> p (u j)"), gate[:], ALU.mult)
                rows = out[P * n0 : P * (n0 + groups), j0 : j0 + width]
                nc.sync.dma_start(
                    rows.rearrange("(u p) j -> p u j", p=P), result[:].rearrange("p (u j) -> p u j", u=groups)
                )

        first_half = []
        for h in range(2):
            features(0, h)
            first_half.append(quantise_a_z(0, BANK * h, BANK, nc.scalar.copy))
        for s in range(PAGES, SLICES):
            place(s)

        for j0, width in PIECES:
            h, c0 = divmod(j0, BANK)
            if c0 == 0:
                features(1, h)
            z_copy = nc.vector.tensor_copy if j0 + width == S else nc.scalar.copy
            second_half = quantise_a_z(1, j0, width, z_copy)
            cols = slice(c0, c0 + width)
            a_mx, z_mx = [
                [(first[0][:, cols], first[1][:, cols]), (second[0][:], second[1][:])]
                for first, second in zip(first_half[h], second_half)
            ]
            second_stage(j0, width, a_mx, z_mx, "first" if h == 1 else "second")
